import numpy as np
import ml_dtypes


def mxq(x, axis, fmt="e4m3"):
    dtype, down = {"e4m3": (ml_dtypes.float8_e4m3fn, 7), "e5m2": (ml_dtypes.float8_e5m2, 14)}[fmt]
    v = np.moveaxis(np.asarray(x, np.float32).astype(ml_dtypes.bfloat16).astype(np.float64), axis, -1)
    blocks = v.reshape(v.shape[:-1] + (-1, 32))
    amax = np.abs(blocks).max(-1, keepdims=True)
    byte = np.maximum(np.where(amax > 0, np.frexp(amax)[1] - 1 + 127, 0) - down, 1)
    scale = np.exp2(byte - 127.0)
    codes = (blocks / scale).astype(np.float32).astype(dtype).astype(np.float64)
    return np.moveaxis((codes * scale).reshape(v.shape), -1, axis)


WIDE = False


def mx_kscale(k):
    if not WIDE:
        return np.ones(k)
    levels = np.array([10, -10, 5, -5, 0])
    if k % 512:
        return np.exp2(np.random.permutation(np.resize(levels, k // 32))).repeat(32)
    a = np.empty((k // 512, 16))
    for p in range(k // 512):
        a[p, :8] = np.random.permutation(np.resize(levels, 8))
        for g in range(8):
            far = levels[np.abs(levels - a[p, g]) >= 10]
            a[p, g + 8] = far[np.random.randint(len(far))]
    return np.exp2(a.ravel()).repeat(32)


BF16 = ml_dtypes.bfloat16


def bf(x):
    return np.asarray(x, np.float32).astype(BF16)


def f64(x):
    return np.asarray(x).astype(np.float64)


E2M1 = np.array([0.0, 0.5, 1.0, 1.5, 2.0, 3.0, 4.0, 6.0, -0.0, -0.5, -1.0, -1.5, -2.0, -3.0, -4.0, -6.0])


def pack_weight(w, fmt):
    k, n = w.shape
    w = f64(bf(w)).reshape(k // 32, 32, n)
    amax = np.abs(w).max(1)
    if fmt == "e4m3":
        byte = np.frexp(amax)[1] - 1 + 127 - 7
    else:
        mant, ex = np.frexp(amax / 6.0)
        byte = np.where(mant > 0.5, ex, ex - 1) + 127
    byte = np.clip(np.where(amax > 0, byte, 1), 1, 254)
    scaled = (w * np.exp2(127.0 - byte)[:, None, :]).reshape(k, n).astype(np.float32)
    by_word = np.ascontiguousarray(scaled.reshape(k // 512, 128, 4, n).transpose(0, 1, 3, 2))
    if fmt == "e4m3":
        words = by_word.astype(ml_dtypes.float8_e4m3fn).view(np.uint8)
    else:
        c = by_word.astype(ml_dtypes.float4_e2m1fn).view(np.uint8) & 0xF
        words = c[..., 0::2] | (c[..., 1::2] << 4)
    return np.ascontiguousarray(words), np.ascontiguousarray(byte.astype(np.uint8).reshape(k // 512, 16, n))


def unpack_weight(words, scales, fmt):
    g, p, n, _ = words.shape
    if fmt == "e4m3":
        vals = np.ascontiguousarray(words).view(ml_dtypes.float8_e4m3fn).astype(np.float64)
    else:
        nib = np.empty((g, p, n, 4), np.uint8)
        nib[..., 0::2] = words & 0xF
        nib[..., 1::2] = words >> 4
        vals = E2M1[nib]
    vals = vals * np.repeat(np.exp2(scales.astype(np.float64) - 127.0), 8, axis=1)[..., None]
    return vals.transpose(0, 1, 3, 2).reshape(g * 512, n)
def pack4(w):
    words, scales = pack_weight(w, "e2m1")
    return words.reshape(words.shape[0], 128, -1), scales


def unpack4(words, scales):
    return unpack_weight(words.reshape(words.shape[0], 128, -1, 2), scales, "e2m1")


def planes(Y):
    n, m = Y.shape
    b = f64(bf(Y)).reshape(n // 32, 32, m)
    amax = np.abs(b).max(1)
    byte = np.clip(np.where(amax > 0, np.frexp(amax)[1] - 1 + 127 - 7, 1), 1, 254)
    codes = (b * np.exp2(127.0 - byte)[:, None, :]).reshape(n, m).astype(np.float32).astype(ml_dtypes.float8_e4m3fn).view(np.uint8)
    words = codes.reshape(n // 512, 128, 4, m).transpose(0, 1, 3, 2)
    return np.ascontiguousarray(words), np.ascontiguousarray(byte.astype(np.uint8).reshape(n // 512, 16, m))


G, T, K, R, P = 4, 768, 1024, 512, 1024


def setup_inputs():
    s = mx_kscale(G * K)
    t = mx_kscale(G * R)
    e = np.exp(0.8 * np.random.randn(G, P))
    context = bf(np.random.randn(G, T, K) * s.reshape(G, 1, K))
    U = np.random.randn(G * K, R) / np.sqrt(K) / s[:, None]
    d = bf(np.exp(0.4 * np.random.randn(G, R)) * t.reshape(G, R))
    V = np.random.randn(G * R, P) / np.sqrt(R) / t[:, None] * np.repeat(e, R, axis=0)
    frames = bf(np.random.randn(G, T, P) * e[:, None, :])
    lo = bf(-0.2 * e * np.exp(0.2 * np.random.randn(G, P)))
    hi = bf(0.3 * e * np.exp(0.2 * np.random.randn(G, P)))
    u_words, u_scales = pack4(U)
    v_words, v_scales = pack4(V)
    return {"context": context, "u_words": u_words, "u_scales": u_scales, "d": d,
            "v_words": v_words, "v_scales": v_scales, "frames": frames, "lo": lo, "hi": hi}

def reference(context, u_words, u_scales, d, v_words, v_scales, frames, lo, hi):
    U = unpack4(u_words, u_scales).reshape(G, K, R)
    V = unpack4(v_words, v_scales).reshape(G, R, P)
    C = mxq(f64(context), 2, "e4m3") @ U
    H = C * f64(d)[:, None, :]
    L = mxq(H, 2, "e4m3") @ V
    D = f64(frames) - L
    y = D - np.minimum(np.maximum(D, f64(lo)[:, None, :]), f64(hi)[:, None, :])
    Y = y.reshape(G * T, P).T
    words, scales = planes(Y)
    return y, words, scales

@@ -1,0 +1,366 @@
+from contextlib import ExitStack
+
+import concourse.mybir as mybir
+from concourse.masks import make_identity
+
+G, T, K, R, NPIX = 4, 768, 1024, 512, 1024
+FLOPS = 2 * G * T * K * R + 2 * G * T * R * NPIX
+
+F32 = mybir.dt.float32
+BF16 = mybir.dt.bfloat16
+I32 = mybir.dt.int32
+U32 = mybir.dt.uint32
+U8 = mybir.dt.uint8
+FP8X4 = mybir.dt.float8_e4m3fn_x4
+FP4X4 = mybir.dt.float4_e2m1fn_x4
+ALU = mybir.AluOpType
+ACT = mybir.ActivationFunctionType
+
+P = 128
+KP = 512
+TILES = G * T // P
+TILES_PER_VIEW = T // P
+PAIR = 2 * P
+PAIRS_PER_VIEW = T // PAIR
+
+
+def tile_lowrank_background_foreground_k7_kernel(
+    tc, context, u_words, u_scales, d, v_words, v_scales, frames, lo, hi, out_0, out_1, out_2
+):
+    nc = tc.nc
+    ctx_rows = context.rearrange("i f k -> (i f) k")
+    frame_rows = frames.rearrange("i f k -> (i f) k")
+    y_rows = out_0.rearrange("i f k -> (i f) k")
+
+    with ExitStack() as stack:
+        keep = stack.enter_context(tc.tile_pool(name="keep", bufs=1))
+        work = stack.enter_context(tc.tile_pool(name="work", bufs=2))
+        psum = stack.enter_context(tc.psum_pool(name="psum", bufs=1))
+        stack.enter_context(tc.manual_schedule())
+
+        def bank(tag):
+            return psum.tile([P, KP], F32, name=tag, tag=tag)
+
+        ident = keep.tile([P, P], F32, name="ident")
+        u_plane = keep.tile([P, 2 * G, R], U8, name="u_plane", align_bytes=64)
+        v_plane = keep.tile([P, G, NPIX], U8, name="v_plane", align_bytes=64)
+        d_rows = keep.tile([P, 16], BF16, name="d_rows")
+        d_sorted = keep.tile([P, G, 2, P], F32, name="d_sorted")
+        bound_rows = keep.tile([P, KP], BF16, name="bound_rows")
+        bound_words = keep.tile([P, 16, 2], F32, name="bound_words")
+        lo_col = keep.tile([P, 32], F32, name="lo_col")
+        neg_hi_col = keep.tile([P, 32], F32, name="neg_hi_col")
+
+        ctx_t, ctx_bank, ctx_q, ctx_codes = {}, {}, {}, {}
+        u_t, v_t, frame_t = {}, {}, {}
+        c_bank, h_sorted, h_bank, h_q, h_codes = {}, {}, {}, {}, {}
+        l_bank, d_t, dt_bank, r_t, yt_t, yb_t, y_bank, y_t = {}, {}, {}, {}, {}, {}, {}, {}
+        y_codes, y_scales = {}, {}
+
+        def load_ctx(x):
+            ctx_t[x] = work.tile([P, K], BF16, name="ctx", tag="ctx", bufs=5)
+            nc.sync.dma_start(out=ctx_t[x][:], in_=ctx_rows[x * P : (x + 1) * P, :])
+
+        def load_u(i):
+            u_t[i] = work.tile([P, 2, 2 * R], U8, name="u", tag="u", bufs=2, align_bytes=64)
+            nc.sync.dma_start(
+                out=u_t[i][:].bitcast(I32),
+                in_=u_words[2 * i : 2 * i + 2].rearrange("g p n -> p g n").bitcast(I32),
+            )
+
+        def load_v(i):
+            v_t[i] = work.tile([P, 2 * NPIX], U8, name="v", tag="v", bufs=2, align_bytes=64)
+            nc.sync.dma_start(out=v_t[i][:].bitcast(I32), in_=v_words[i].bitcast(I32))
+
+        def load_frames(n):
+            frame_t[n] = work.tile([P, 2, NPIX], BF16, name="frames", tag="frames", bufs=3)
+            nc.sync.dma_start(
+                out=frame_t[n][:],
+                in_=frame_rows[n * PAIR : (n + 1) * PAIR, :].rearrange("(j m) c -> m j c", j=2),
+            )
+
+        def load_plane(plane, scales):
+            for q in range(4):
+                nc.sync.dma_start(
+                    out=plane[32 * q : 32 * q + 4].bitcast(I32),
+                    in_=scales[:, 4 * q : 4 * q + 4, :].rearrange("g r n -> r g n").bitcast(I32),
+                )
+
+        def turn_ctx(x):
+            ctx_bank[x] = bank("turn")
+            words = ctx_t[x][:].bitcast(F32)
+            for g in range(2):
+                for u in range(2):
+                    c0 = (2 * g + u) * P
+                    nc.tensor.transpose(
+                        ctx_bank[x][:, c0 : c0 + P], words[:, 256 * g + u : 256 * (g + 1) : 2], ident[:]
+                    )
+
+        def copy_ctx(x):
+            ctx_q[x] = work.tile([P, K], BF16, name="ctx_q", tag="ctx_q", bufs=2, align_bytes=64)
+            nc.scalar.copy(
+                out=ctx_q[x][:].bitcast(F32).rearrange("p (g m u) -> p g m u", g=2, u=2),
+                in_=ctx_bank[x][:].rearrange("p (g u m) -> p g m u", g=2, u=2),
+            )
+
+        def quantize_ctx(x):
+            codes = work.tile([P, 2 * P], U32, name="ctx_codes", tag="ctx_codes", bufs=3, align_bytes=64)
+            scales = work.tile([P, 2 * P], U8, name="ctx_scales", tag="ctx_scales", bufs=3, align_bytes=64)
+            ctx_codes[x] = (codes, scales)
+            nc.vector.quantize_mx(out=codes[:].bitcast(FP8X4), scales=scales[:], in_=ctx_q[x][:])
+
+        def stage1(x):
+            i = x // TILES_PER_VIEW
+            codes, scales = ctx_codes[x]
+            c_bank[x] = bank("coef")
+            for g in range(2):
+                nc.tensor.matmul_mx(
+                    out=c_bank[x][:],
+                    lhsT=codes[:, g * P : (g + 1) * P].bitcast(FP8X4),
+                    lhsT_scale=scales[:, g * P : (g + 1) * P],
+                    rhs=u_t[i][:, g, :].bitcast(FP4X4),
+                    rhs_scale=u_plane[:, 2 * i + g, :],
+                    start=(g == 0),
+                    stop=(g == 1),
+                )
+
+        def weigh(x):
+            i = x // TILES_PER_VIEW
+            h_sorted[x] = work.tile([P, R], BF16, name="h_sorted", tag="h_sorted", bufs=2)
+            nc.vector.tensor_tensor(
+                out=h_sorted[x][:].rearrange("m (u p e) -> m u p e", u=2, e=2),
+                in0=c_bank[x][:].rearrange("m (p u e) -> m u p e", u=2, e=2),
+                in1=d_sorted[:, i].rearrange("m u p -> m (u p)").bitcast(BF16).rearrange("m (u p e) -> m u p e", u=2, e=2),
+                op=ALU.mult,
+            )
+
+        def turn_h(x):
+            h_bank[x] = bank("turn")
+            words = h_sorted[x][:].bitcast(F32)
+            for u in range(2):
+                nc.tensor.transpose(h_bank[x][:, u * P : (u + 1) * P], words[:, u * P : (u + 1) * P], ident[:])
+
+        def copy_h(x):
+            h_q[x] = work.tile([P, R], BF16, name="h_q", tag="h_q", bufs=2, align_bytes=64)
+            nc.scalar.copy(
+                out=h_q[x][:].bitcast(F32).rearrange("p (m u) -> p m u", u=2),
+                in_=h_bank[x][:, : 2 * P].rearrange("p (u m) -> p m u", u=2),
+            )
+
+        def quantize_h(x):
+            codes = work.tile([P, P], U32, name="h_codes", tag="h_codes", bufs=6, align_bytes=64)
+            scales = work.tile([P, P], U8, name="h_scales", tag="h_scales", bufs=6, align_bytes=64)
+            h_codes[x] = (codes, scales)
+            nc.vector.quantize_mx(out=codes[:].bitcast(FP8X4), scales=scales[:], in_=h_q[x][:])
+
+        def stage2(s):
+            n, g = divmod(s, 2)
+            i = n // PAIRS_PER_VIEW
+            for j in range(2):
+                codes, scales = h_codes[2 * n + j]
+                l_bank[s, j] = bank("back%d" % j)
+                nc.tensor.matmul_mx(
+                    out=l_bank[s, j][:],
+                    lhsT=codes[:].bitcast(FP8X4),
+                    lhsT_scale=scales[:],
+                    rhs=v_t[i][:, 2 * KP * g : 2 * KP * (g + 1)].bitcast(FP4X4),
+                    rhs_scale=v_plane[:, i, KP * g : KP * (g + 1)],
+                    start=True,
+                    stop=True,
+                )
+
+        def residual(s):
+            n, g = divmod(s, 2)
+            d_t[s] = work.tile([P, 2, KP], F32, name="resid", tag="resid", bufs=3)
+            for j in range(2):
+                nc.vector.tensor_tensor(
+                    out=d_t[s][:, j, :].rearrange("m (t p) -> m t p", t=4),
+                    in0=frame_t[n][:, j, KP * g : KP * (g + 1)].rearrange("m (p t) -> m t p", t=4),
+                    in1=l_bank[s, j][:].rearrange("m (p t) -> m t p", t=4),
+                    op=ALU.subtract,
+                )
+
+        def turn_residual(s):
+            for h in range(2):
+                dt_bank[s, h] = bank("resid%d" % h)
+                for tt in range(2):
+                    t = 2 * h + tt
+                    for j in range(2):
+                        c0 = tt * PAIR + j * P
+                        nc.tensor.transpose(
+                            dt_bank[s, h][:, c0 : c0 + P], d_t[s][:, j, t * P : (t + 1) * P], ident[:]
+                        )
+
+        def bound_col(s, t):
+            n, g = divmod(s, 2)
+            c = (2 * (n // PAIRS_PER_VIEW) + g) * 4 + t
+            return slice(c, c + 1)
+
+        def above(s):
+            r_t[s] = work.tile([P, 4, PAIR], F32, name="above", tag="above", bufs=2)
+            for t in range(4):
+                h, tt = divmod(t, 2)
+                nc.scalar.activation(
+                    out=r_t[s][:, t, :],
+                    in_=dt_bank[s, h][:, tt * PAIR : (tt + 1) * PAIR],
+                    func=ACT.Relu,
+                    bias=neg_hi_col[:, bound_col(s, t)],
+                )
+
+        def threshold(s):
+            yt_t[s] = work.tile([P, 4, PAIR], F32, name="yt", tag="yt", bufs=3)
+            for t in range(4):
+                h, tt = divmod(t, 2)
+                nc.vector.scalar_tensor_tensor(
+                    out=yt_t[s][:, t, :],
+                    in0=dt_bank[s, h][:, tt * PAIR : (tt + 1) * PAIR],
+                    scalar=lo_col[:, bound_col(s, t)],
+                    in1=r_t[s][:, t, :],
+                    op0=ALU.subtract,
+                    op1=ALU.min,
+                )
+
+        def round_y(s):
+            yb_t[s] = work.tile([P, 4 * PAIR], BF16, name="yb", tag="yb", bufs=2, align_bytes=64)
+            nc.gpsimd.tensor_scalar(
+                out=yb_t[s][:].rearrange("p (m t) -> p m t", t=4),
+                in0=yt_t[s][:].rearrange("p t m -> p m t"),
+                scalar1=1.0,
+                scalar2=1.0,
+                op0=ALU.mult,
+                op1=ALU.mult,
+            )
+
+        def quantize_y(s):
+            n, g = divmod(s, 2)
+            i, k = divmod(n, PAIRS_PER_VIEW)
+            if g == 0:
+                y_codes[n] = work.tile([P, 2, PAIR], U32, name="y_codes", tag="y_codes", bufs=3, align_bytes=64)
+                if k == 0:
+                    y_scales[i] = work.tile([P, 2, T], U8, name="y_scales", tag="y_scales", bufs=2, align_bytes=64)
+            nc.vector.quantize_mx(
+                out=y_codes[n][:, g, :].bitcast(FP8X4),
+                scales=y_scales[i][:, g, k * PAIR : (k + 1) * PAIR],
+                in_=yb_t[s][:],
+            )
+
+        def turn_y(s):
+            for j in range(2):
+                y_bank[s, j] = bank("out%d" % j)
+                for t in range(4):
+                    nc.tensor.transpose(
+                        y_bank[s, j][:, t * P : (t + 1) * P], yt_t[s][:, t, j * P : (j + 1) * P], ident[:]
+                    )
+
+        def copy_y(s):
+            n, g = divmod(s, 2)
+            if g == 0:
+                y_t[n] = work.tile([P, 2, NPIX], F32, name="y", tag="y", bufs=3)
+            for j in range(2):
+                nc.scalar.copy(
+                    out=y_t[n][:, j, KP * g : KP * (g + 1)].rearrange("m (p t) -> m p t", t=4),
+                    in_=y_bank[s, j][:].rearrange("m (t p) -> m p t", t=4),
+                )
+
+        def store_y(s):
+            n, g = divmod(s, 2)
+            rows = y_rows[n * PAIR : (n + 1) * PAIR, :].rearrange("(j m) c -> m j c", j=2)
+            if n == TILES // 2 - 1:
+                cols = slice(KP * g, KP * (g + 1))
+                nc.sync.dma_start(out=rows[:, :, cols], in_=y_t[n][:, :, cols])
+            elif g == 1:
+                nc.sync.dma_start(out=rows, in_=y_t[n][:])
+
+        def store_planes(s):
+            n, g = divmod(s, 2)
+            i, k = divmod(n, PAIRS_PER_VIEW)
+            if g == 0:
+                return
+            nc.sync.dma_start(
+                out=out_1[:, :, n * PAIR : (n + 1) * PAIR, :].rearrange("g p m t -> p g (m t)").bitcast(I32),
+                in_=y_codes[n][:].bitcast(I32),
+            )
+            if k == PAIRS_PER_VIEW - 1:
+                for q in range(4):
+                    nc.sync.dma_start(
+                        out=out_2[:, 4 * q : 4 * q + 4, i * T : (i + 1) * T].rearrange("g r m -> r g m").bitcast(I32),
+                        in_=y_scales[i][32 * q : 32 * q + 4].bitcast(I32),
+                    )
+
+        def spread_d():
+            words = d_rows[:].bitcast(F32)
+            for u in range(2):
+                b = bank("resid%d" % u)
+                for a in range(4):
+                    c = 2 * a + u
+                    nc.tensor.transpose(b[:, a * P : (a + 1) * P], words[:, c : c + 1].to_broadcast([P, P]), ident[:])
+                nc.vector.tensor_copy(
+                    out=d_sorted[:, :, u, :].rearrange("q i (b a) -> q i b a", a=4),
+                    in_=b[:].rearrange("q (a i b) -> q i b a", a=4, i=G),
+                )
+
+        def turn_bounds():
+            words = bound_rows[:].bitcast(F32)
+            b = bank("out0")
+            for u in range(2):
+                nc.tensor.transpose(b[:, u * P : (u + 1) * P], words[:, u : 256 : 2], ident[:])
+            nc.vector.tensor_copy(
+                out=bound_words[:], in_=b[:, : 2 * P].rearrange("p (u r) -> p r u", u=2)[:, :16, :]
+            )
+            values = bound_words[:].rearrange("p r u -> p (r u)").bitcast(BF16)
+            nc.vector.tensor_copy(out=lo_col[:], in_=values[:, :32])
+            nc.vector.tensor_scalar(
+                out=neg_hi_col[:], in0=values[:, 32:], scalar1=-1.0, scalar2=None, op0=ALU.mult
+            )
+
+        make_identity(nc, ident[:])
+        nc.vector.memset(u_plane[:].bitcast(I32), 0)
+        nc.vector.memset(v_plane[:].bitcast(I32), 0)
+        nc.vector.memset(bound_rows[:], 0.0)
+
+        load_ctx(0)
+        nc.sync.dma_start(out=d_rows[:], in_=d.rearrange("i (b c) -> (i b) c", c=16))
+        load_plane(u_plane, u_scales)
+        load_u(0)
+        load_ctx(1)
+        load_ctx(2)
+        load_plane(v_plane, v_scales)
+        nc.sync.dma_start(out=bound_rows[0:8, :], in_=lo.rearrange("i (g c) -> (i g) c", g=2))
+        nc.sync.dma_start(out=bound_rows[8:16, :], in_=hi.rearrange("i (g c) -> (i g) c", g=2))
+        load_v(0)
+
+        def when(f, x):
+            if 0 <= x < TILES:
+                f(x)
+
+        for s in range(-8, TILES + 2):
+            when(stage2, s + 2)
+            when(threshold, s)
+            when(copy_ctx, s + 7)
+            when(turn_y, s - 1)
+            when(turn_h, s + 5)
+            when(copy_y, s - 1)
+            when(copy_h, s + 5)
+            when(round_y, s)
+            when(stage1, s + 6)
+            when(residual, s + 2)
+            when(weigh, s + 6)
+            when(turn_residual, s + 1)
+            when(turn_ctx, s + 8)
+            if s == -8:
+                spread_d()
+            if s == -5:
+                turn_bounds()
+            when(above, s + 1)
+            when(quantize_ctx, s + 7)
+            when(quantize_h, s + 5)
+            when(quantize_y, s)
+            when(load_ctx, s + 11)
+            if (s + 6) % 2 == 0 and 0 <= s + 6 < TILES:
+                load_frames((s + 6) // 2)
+            if (s + 10) % TILES_PER_VIEW == 0 and 0 < s + 10 < TILES:
+                load_u((s + 10) // TILES_PER_VIEW)
+            if (s + 6) % TILES_PER_VIEW == 0 and 0 < s + 6 < TILES:
+                load_v((s + 6) // TILES_PER_VIEW)
+            when(store_planes, s - 1)
+            when(store_y, s - 1)

@@ -47,7 +47,6 @@ def tile_lowrank_background_foreground_k7_kernel(
         d_rows = keep.tile([P, 16], BF16, name="d_rows")
         d_sorted = keep.tile([P, G, 2, P], F32, name="d_sorted")
         bound_rows = keep.tile([P, KP], BF16, name="bound_rows")
-        bound_words = keep.tile([P, 16, 2], F32, name="bound_words")
         lo_col = keep.tile([P, 32], F32, name="lo_col")
         neg_hi_col = keep.tile([P, 32], F32, name="neg_hi_col")
 
@@ -86,15 +85,15 @@ def tile_lowrank_background_foreground_k7_kernel(
                     in_=scales[:, 4 * q : 4 * q + 4, :].rearrange("g r n -> r g n").bitcast(I32),
                 )
 
-        def turn_ctx(x):
-            ctx_bank[x] = bank("turn")
+        def turn_ctx(x, g, tag="turn"):
+            if g == 0:
+                ctx_bank[x] = bank(tag)
             words = ctx_t[x][:].bitcast(F32)
-            for g in range(2):
-                for u in range(2):
-                    c0 = (2 * g + u) * P
-                    nc.tensor.transpose(
-                        ctx_bank[x][:, c0 : c0 + P], words[:, 256 * g + u : 256 * (g + 1) : 2], ident[:]
-                    )
+            for u in range(2):
+                c0 = (2 * g + u) * P
+                nc.tensor.transpose(
+                    ctx_bank[x][:, c0 : c0 + P], words[:, 256 * g + u : 256 * (g + 1) : 2], ident[:]
+                )
 
         def copy_ctx(x):
             ctx_q[x] = work.tile([P, K], BF16, name="ctx_q", tag="ctx_q", bufs=2, align_bytes=64)
@@ -109,10 +108,10 @@ def tile_lowrank_background_foreground_k7_kernel(
             ctx_codes[x] = (codes, scales)
             nc.vector.quantize_mx(out=codes[:].bitcast(FP8X4), scales=scales[:], in_=ctx_q[x][:])
 
-        def stage1(x):
+        def stage1(x, tag="coef"):
             i = x // TILES_PER_VIEW
             codes, scales = ctx_codes[x]
-            c_bank[x] = bank("coef")
+            c_bank[x] = bank(tag)
             for g in range(2):
                 nc.tensor.matmul_mx(
                     out=c_bank[x][:],
@@ -134,8 +133,8 @@ def tile_lowrank_background_foreground_k7_kernel(
                 op=ALU.mult,
             )
 
-        def turn_h(x):
-            h_bank[x] = bank("turn")
+        def turn_h(x, tag="coef"):
+            h_bank[x] = bank(tag)
             words = h_sorted[x][:].bitcast(F32)
             for u in range(2):
                 nc.tensor.transpose(h_bank[x][:, u * P : (u + 1) * P], words[:, u * P : (u + 1) * P], ident[:])
@@ -196,10 +195,11 @@ def tile_lowrank_background_foreground_k7_kernel(
             c = (2 * (n // PAIRS_PER_VIEW) + g) * 4 + t
             return slice(c, c + 1)
 
-        def above(s):
-            r_t[s] = work.tile([P, 4, PAIR], F32, name="above", tag="above", bufs=2)
-            for t in range(4):
-                h, tt = divmod(t, 2)
+        def above(s, h):
+            if h == 0:
+                r_t[s] = work.tile([P, 4, PAIR], F32, name="above", tag="above", bufs=2)
+            for tt in range(2):
+                t = 2 * h + tt
                 nc.scalar.activation(
                     out=r_t[s][:, t, :],
                     in_=dt_bank[s, h][:, tt * PAIR : (tt + 1) * PAIR],
@@ -221,7 +221,14 @@ def tile_lowrank_background_foreground_k7_kernel(
                 )
 
         def round_y(s):
-            yb_t[s] = work.tile([P, 4 * PAIR], BF16, name="yb", tag="yb", bufs=2, align_bytes=64)
+            if s == TILES - 1:
+                yb_t[s] = keep.tile([P, 4 * PAIR], BF16, name="yb_last", align_bytes=64)
+                nc.vector.tensor_copy(
+                    out=yb_t[s][:].rearrange("p (c i t) -> p c t i", t=4, i=4),
+                    in_=yt_t[s][:].rearrange("p t (c i) -> p c t i", i=4),
+                )
+                return
+            yb_t[s] = work.tile([P, 4 * PAIR], BF16, name="yb", tag="yb", bufs=1, align_bytes=64)
             nc.gpsimd.tensor_scalar(
                 out=yb_t[s][:].rearrange("p (m t) -> p m t", t=4),
                 in0=yt_t[s][:].rearrange("p t m -> p m t"),
@@ -265,102 +272,185 @@ def tile_lowrank_background_foreground_k7_kernel(
         def store_y(s):
             n, g = divmod(s, 2)
             rows = y_rows[n * PAIR : (n + 1) * PAIR, :].rearrange("(j m) c -> m j c", j=2)
-            if n == TILES // 2 - 1:
-                cols = slice(KP * g, KP * (g + 1))
+            cols = slice(KP * g, KP * (g + 1))
+            if s == TILES - 1:
+                for j in range(2):
+                    nc.sync.dma_start(out=rows[:, j, cols], in_=y_t[n][:, j, cols])
+            else:
                 nc.sync.dma_start(out=rows[:, :, cols], in_=y_t[n][:, :, cols])
-            elif g == 1:
-                nc.sync.dma_start(out=rows, in_=y_t[n][:])
 
         def store_planes(s):
             n, g = divmod(s, 2)
             i, k = divmod(n, PAIRS_PER_VIEW)
-            if g == 0:
-                return
-            nc.sync.dma_start(
-                out=out_1[:, :, n * PAIR : (n + 1) * PAIR, :].rearrange("g p m t -> p g (m t)").bitcast(I32),
-                in_=y_codes[n][:].bitcast(I32),
-            )
-            if k == PAIRS_PER_VIEW - 1:
+            words = out_1[:, :, n * PAIR : (n + 1) * PAIR, :].rearrange("g p m t -> p g (m t)").bitcast(I32)
+            if n == TILES // 2 - 1:
+                nc.sync.dma_start(out=words[:, g, :], in_=y_codes[n][:, g, :].bitcast(I32))
+            elif g == 1:
+                nc.sync.dma_start(out=words, in_=y_codes[n][:].bitcast(I32))
+            if g == 1 and k == PAIRS_PER_VIEW - 1:
                 for q in range(4):
                     nc.sync.dma_start(
                         out=out_2[:, 4 * q : 4 * q + 4, i * T : (i + 1) * T].rearrange("g r m -> r g m").bitcast(I32),
                         in_=y_scales[i][32 * q : 32 * q + 4].bitcast(I32),
                     )
 
-        def spread_d():
+        def spread_d(u):
             words = d_rows[:].bitcast(F32)
-            for u in range(2):
-                b = bank("resid%d" % u)
+            if True:
+                b = bank("out%d" % u)
                 for a in range(4):
                     c = 2 * a + u
                     nc.tensor.transpose(b[:, a * P : (a + 1) * P], words[:, c : c + 1].to_broadcast([P, P]), ident[:])
-                nc.vector.tensor_copy(
+                nc.scalar.copy(
                     out=d_sorted[:, :, u, :].rearrange("q i (b a) -> q i b a", a=4),
                     in_=b[:].rearrange("q (a i b) -> q i b a", a=4, i=G),
                 )
 
         def turn_bounds():
             words = bound_rows[:].bitcast(F32)
-            b = bank("out0")
+            b = bank("out1")
             for u in range(2):
                 nc.tensor.transpose(b[:, u * P : (u + 1) * P], words[:, u : 256 : 2], ident[:])
-            nc.vector.tensor_copy(
-                out=bound_words[:], in_=b[:, : 2 * P].rearrange("p (u r) -> p r u", u=2)[:, :16, :]
+            values = b[:, : 2 * P].bitcast(BF16).rearrange("p (u r e) -> p r u e", u=2, e=2)
+            nc.scalar.activation(
+                out=neg_hi_col[:].rearrange("p (r u e) -> p r u e", u=2, e=2),
+                in_=values[:, 8:16], func=ACT.Identity, scale=-1.0,
             )
-            values = bound_words[:].rearrange("p r u -> p (r u)").bitcast(BF16)
-            nc.vector.tensor_copy(out=lo_col[:], in_=values[:, :32])
-            nc.vector.tensor_scalar(
-                out=neg_hi_col[:], in0=values[:, 32:], scalar1=-1.0, scalar2=None, op0=ALU.mult
+            nc.scalar.activation(
+                out=lo_col[:].rearrange("p (r u e) -> p r u e", u=2, e=2), in_=values[:, 0:8], func=ACT.Identity
             )
 
+        nc.vector.memset(bound_rows[:], 0.0)
         make_identity(nc, ident[:])
         nc.vector.memset(u_plane[:].bitcast(I32), 0)
         nc.vector.memset(v_plane[:].bitcast(I32), 0)
-        nc.vector.memset(bound_rows[:], 0.0)
 
+        def load_d():
+            nc.sync.dma_start(out=d_rows[:], in_=d.rearrange("i (b c) -> (i b) c", c=16))
+
+        def load_bounds():
+            nc.sync.dma_start(out=bound_rows[0:8, :], in_=lo.rearrange("i (g c) -> (i g) c", g=2))
+            nc.sync.dma_start(out=bound_rows[8:16, :], in_=hi.rearrange("i (g c) -> (i g) c", g=2))
+
+        def when(f, x, *more):
+            if 0 <= x < TILES:
+                f(x, *more)
+
+        def prepare_ctx(x, tag):
+            turn_ctx(x, 0, tag)
+            turn_ctx(x, 1)
+            copy_ctx(x)
+            quantize_ctx(x)
+
+        def finish_h(x, tag):
+            turn_h(x, tag)
+            copy_h(x)
+            quantize_h(x)
+
+        load_d()
+        load_bounds()
         load_ctx(0)
-        nc.sync.dma_start(out=d_rows[:], in_=d.rearrange("i (b c) -> (i b) c", c=16))
+        load_ctx(1)
         load_plane(u_plane, u_scales)
         load_u(0)
-        load_ctx(1)
         load_ctx(2)
+        load_ctx(3)
         load_plane(v_plane, v_scales)
-        nc.sync.dma_start(out=bound_rows[0:8, :], in_=lo.rearrange("i (g c) -> (i g) c", g=2))
-        nc.sync.dma_start(out=bound_rows[8:16, :], in_=hi.rearrange("i (g c) -> (i g) c", g=2))
         load_v(0)
+        load_ctx(4)
+        load_frames(0)
 
-        def when(f, x):
-            if 0 <= x < TILES:
-                f(x)
+        turn_bounds()
+        prepare_ctx(0, "turn")
+        spread_d(0)
+        prepare_ctx(1, "resid0")
+        stage1(0, "coef")
+        spread_d(1)
+        turn_ctx(2, 0, "turn")
+        turn_ctx(2, 1)
+        load_ctx(5)
+        stage1(1, "back0")
+        weigh(0)
+        copy_ctx(2)
+        quantize_ctx(2)
+        turn_h(0, "out0")
+        turn_ctx(3, 0, "resid0")
+        turn_ctx(3, 1)
+        load_ctx(6)
+        load_frames(1)
+        weigh(1)
+        copy_h(0)
+        quantize_h(0)
+        copy_ctx(3)
+        quantize_ctx(3)
+        stage1(2, "coef")
+        turn_h(1, "out0")
+        turn_ctx(4, 0, "turn")
+        turn_ctx(4, 1)
+        load_ctx(7)
+        weigh(2)
+        copy_h(1)
+        quantize_h(1)
+        copy_ctx(4)
+        quantize_ctx(4)
+        stage1(3, "out1")
+        stage2(0)
+        turn_h(2, "out0")
+        turn_ctx(5, 0, "turn")
+        turn_ctx(5, 1)
+        load_ctx(8)
+        load_u(1)
+        load_frames(2)
+        residual(0)
+        weigh(3)
+        copy_h(2)
+        copy_ctx(5)
+        stage1(4)
+        stage2(1)
+        turn_residual(0)
+        turn_h(3, "out1")
+        turn_ctx(6, 0)
+        above(0, 0)
+        copy_h(3)
+        above(0, 1)
+        quantize_h(2)
+        residual(1)
+        quantize_h(3)
+        quantize_ctx(5)
 
-        for s in range(-8, TILES + 2):
-            when(stage2, s + 2)
+        for s in range(TILES):
             when(threshold, s)
-            when(copy_ctx, s + 7)
+            when(round_y, s - 1)
             when(turn_y, s - 1)
-            when(turn_h, s + 5)
+            when(turn_ctx, s + 6, 1)
             when(copy_y, s - 1)
-            when(copy_h, s + 5)
-            when(round_y, s)
-            when(stage1, s + 6)
+            when(weigh, s + 4)
+            when(stage2, s + 2)
+            when(copy_ctx, s + 6)
+            when(turn_h, s + 4)
+            when(copy_h, s + 4)
             when(residual, s + 2)
-            when(weigh, s + 6)
             when(turn_residual, s + 1)
-            when(turn_ctx, s + 8)
-            if s == -8:
-                spread_d()
-            if s == -5:
-                turn_bounds()
-            when(above, s + 1)
-            when(quantize_ctx, s + 7)
-            when(quantize_h, s + 5)
-            when(quantize_y, s)
-            when(load_ctx, s + 11)
-            if (s + 6) % 2 == 0 and 0 <= s + 6 < TILES:
+            when(turn_ctx, s + 7, 0)
+            when(above, s + 1, 0)
+            when(above, s + 1, 1)
+            when(quantize_h, s + 4)
+            when(quantize_ctx, s + 6)
+            when(quantize_y, s - 1)
+            when(stage1, s + 5)
+            when(load_ctx, s + 9)
+            if s % 2 == 0 and s + 6 < TILES:
                 load_frames((s + 6) // 2)
-            if (s + 10) % TILES_PER_VIEW == 0 and 0 < s + 10 < TILES:
-                load_u((s + 10) // TILES_PER_VIEW)
-            if (s + 6) % TILES_PER_VIEW == 0 and 0 < s + 6 < TILES:
+            if (s + 9) % TILES_PER_VIEW == 0 and s + 9 < TILES:
+                load_u((s + 9) // TILES_PER_VIEW)
+            if (s + 6) % TILES_PER_VIEW == 0 and s + 6 < TILES:
                 load_v((s + 6) // TILES_PER_VIEW)
-            when(store_planes, s - 1)
             when(store_y, s - 1)
+            when(store_planes, s - 1)
+        last = TILES - 1
+        turn_y(last)
+        round_y(last)
+        copy_y(last)
+        quantize_y(last)
+        store_y(last)
+        store_planes(last)

@@ -17,11 +17,22 @@ ALU = mybir.AluOpType
 ACT = mybir.ActivationFunctionType
 
 P = 128
-KP = 512
+GROUP = 512
+SLOTS = 4
+UNIT_FRAMES = 2 * P
 TILES = G * T // P
+UNITS = TILES
 TILES_PER_VIEW = T // P
-PAIR = 2 * P
-PAIRS_PER_VIEW = T // PAIR
+PAIRS_PER_VIEW = T // UNIT_FRAMES
+BOUND_ROWS = 2 * G
+
+SHARED_UNITS = 19
+SHARE_PERIOD = 4
+
+TURN, COEF = "turn", "coef"
+BACK = ("back0", "back1")
+RESID = ("resid0", "resid1")
+OUT = ("out0", "out1")
 
 
 def tile_lowrank_background_foreground_k7_kernel(
@@ -38,86 +49,129 @@ def tile_lowrank_background_foreground_k7_kernel(
         psum = stack.enter_context(tc.psum_pool(name="psum", bufs=1))
         stack.enter_context(tc.manual_schedule())
 
-        def bank(tag):
-            return psum.tile([P, KP], F32, name=tag, tag=tag)
+        def bank(role):
+            return psum.tile([P, GROUP], F32, name=role, tag=role)
 
         ident = keep.tile([P, P], F32, name="ident")
         u_plane = keep.tile([P, 2 * G, R], U8, name="u_plane", align_bytes=64)
         v_plane = keep.tile([P, G, NPIX], U8, name="v_plane", align_bytes=64)
-        d_rows = keep.tile([P, 16], BF16, name="d_rows")
+        d_first = keep.tile([P, 1, SLOTS], BF16, name="d_first")
+        d_rest = keep.tile([P, G - 1, SLOTS], BF16, name="d_rest")
         d_sorted = keep.tile([P, G, 2, P], F32, name="d_sorted")
-        bound_rows = keep.tile([P, KP], BF16, name="bound_rows")
-        lo_col = keep.tile([P, 32], F32, name="lo_col")
-        neg_hi_col = keep.tile([P, 32], F32, name="neg_hi_col")
+        bound_rows = keep.tile([P, GROUP], BF16, name="bound_rows")
+        lo_col = keep.tile([P, BOUND_ROWS * SLOTS], F32, name="lo_col")
+        neg_hi_col = keep.tile([P, BOUND_ROWS * SLOTS], F32, name="neg_hi_col")
 
-        ctx_t, ctx_bank, ctx_q, ctx_codes = {}, {}, {}, {}
-        u_t, v_t, frame_t = {}, {}, {}
-        c_bank, h_sorted, h_bank, h_q, h_codes = {}, {}, {}, {}, {}
-        l_bank, d_t, dt_bank, r_t, yt_t, yb_t, y_bank, y_t = {}, {}, {}, {}, {}, {}, {}, {}
-        y_codes, y_scales = {}, {}
+        ctx_raw, ctx_bank, ctx_words, ctx_mx = {}, {}, {}, {}
+        u_codes, v_codes, frame_pair = {}, {}, {}
+        coef_bank, h_sorted, h_bank, h_words, h_mx = {}, {}, {}, {}, {}
+        back_bank, resid, resid_bank, above_hi, below_lo = {}, {}, {}, {}, {}
+        y_turned, y_words, out_bank, y_pair, y_codes, y_scales = {}, {}, {}, {}, {}, {}
 
         def load_ctx(x):
-            ctx_t[x] = work.tile([P, K], BF16, name="ctx", tag="ctx", bufs=5)
-            nc.sync.dma_start(out=ctx_t[x][:], in_=ctx_rows[x * P : (x + 1) * P, :])
+            ctx_raw[x] = work.tile([P, K], BF16, name="ctx", tag="ctx", bufs=5)
+            nc.sync.dma_start(out=ctx_raw[x][:], in_=ctx_rows[x * P : (x + 1) * P, :])
 
         def load_u(i):
-            u_t[i] = work.tile([P, 2, 2 * R], U8, name="u", tag="u", bufs=2, align_bytes=64)
+            u_codes[i] = work.tile([P, 2, 2 * R], U8, name="u", tag="u", bufs=2, align_bytes=64)
             nc.sync.dma_start(
-                out=u_t[i][:].bitcast(I32),
+                out=u_codes[i][:].bitcast(I32),
                 in_=u_words[2 * i : 2 * i + 2].rearrange("g p n -> p g n").bitcast(I32),
             )
 
         def load_v(i):
-            v_t[i] = work.tile([P, 2 * NPIX], U8, name="v", tag="v", bufs=2, align_bytes=64)
-            nc.sync.dma_start(out=v_t[i][:].bitcast(I32), in_=v_words[i].bitcast(I32))
+            v_codes[i] = work.tile([P, 2 * NPIX], U8, name="v", tag="v", bufs=2, align_bytes=64)
+            nc.sync.dma_start(out=v_codes[i][:].bitcast(I32), in_=v_words[i].bitcast(I32))
 
         def load_frames(n):
-            frame_t[n] = work.tile([P, 2, NPIX], BF16, name="frames", tag="frames", bufs=3)
+            frame_pair[n] = work.tile([P, 2, NPIX], BF16, name="frames", tag="frames", bufs=3)
             nc.sync.dma_start(
-                out=frame_t[n][:],
-                in_=frame_rows[n * PAIR : (n + 1) * PAIR, :].rearrange("(j m) c -> m j c", j=2),
+                out=frame_pair[n][:],
+                in_=frame_rows[n * UNIT_FRAMES : (n + 1) * UNIT_FRAMES, :].rearrange("(j m) c -> m j c", j=2),
             )
 
         def load_plane(plane, scales):
-            for q in range(4):
+            for quad in range(4):
                 nc.sync.dma_start(
-                    out=plane[32 * q : 32 * q + 4].bitcast(I32),
-                    in_=scales[:, 4 * q : 4 * q + 4, :].rearrange("g r n -> r g n").bitcast(I32),
+                    out=plane[32 * quad : 32 * quad + 4].bitcast(I32),
+                    in_=scales[:, 4 * quad : 4 * quad + 4, :].rearrange("g r n -> r g n").bitcast(I32),
                 )
 
-        def turn_ctx(x, g, tag="turn"):
-            if g == 0:
-                ctx_bank[x] = bank(tag)
-            words = ctx_t[x][:].bitcast(F32)
+        def load_d(rows, views):
+            nc.sync.dma_start(out=rows[:], in_=d[views].rearrange("i (p c) -> p i c", c=SLOTS))
+
+        def load_bounds():
+            nc.sync.dma_start(out=bound_rows[:BOUND_ROWS, :], in_=lo.rearrange("i (g c) -> (i g) c", g=2))
+            nc.sync.dma_start(
+                out=bound_rows[BOUND_ROWS : 2 * BOUND_ROWS, :], in_=hi.rearrange("i (g c) -> (i g) c", g=2)
+            )
+
+        def spread_d(view, count, rows, first_row, role):
+            pairs = rows[:].rearrange("p i c -> p (i c)").bitcast(F32)
+            spread = bank(role)
+            for c in range(2 * count):
+                w = 2 * first_row + c
+                nc.tensor.transpose(spread[:, c * P : (c + 1) * P], pairs[:, w : w + 1].to_broadcast([P, P]), ident[:])
+            nc.scalar.copy(
+                out=d_sorted[:, view : view + count].rearrange("q i u p -> q (i u p)"), in_=spread[:, : 2 * count * P]
+            )
+
+        def turn_bounds():
+            pairs = bound_rows[:].bitcast(F32)
+            turned = bank(OUT[1])
             for u in range(2):
-                c0 = (2 * g + u) * P
-                nc.tensor.transpose(
-                    ctx_bank[x][:, c0 : c0 + P], words[:, 256 * g + u : 256 * (g + 1) : 2], ident[:]
-                )
+                nc.tensor.transpose(turned[:, u * P : (u + 1) * P], pairs[:, u : GROUP // 2 : 2], ident[:])
+            values = turned[:, : 2 * P].bitcast(BF16).rearrange("p (u r e) -> p r u e", u=2, e=2)
+            nc.scalar.activation(
+                out=neg_hi_col[:].rearrange("p (r u e) -> p r u e", u=2, e=2),
+                in_=values[:, BOUND_ROWS : 2 * BOUND_ROWS],
+                func=ACT.Identity,
+                scale=-1.0,
+            )
+            nc.scalar.activation(
+                out=lo_col[:].rearrange("p (r u e) -> p r u e", u=2, e=2),
+                in_=values[:, :BOUND_ROWS],
+                func=ACT.Identity,
+            )
+
+        def turn_ctx(x, role=TURN):
+            ctx_bank[x] = bank(role)
+            pairs = ctx_raw[x][:].bitcast(F32)
+            for g in range(2):
+                for u in range(2):
+                    c0 = (2 * g + u) * P
+                    nc.tensor.transpose(
+                        ctx_bank[x][:, c0 : c0 + P], pairs[:, 2 * P * g + u : 2 * P * (g + 1) : 2], ident[:]
+                    )
 
         def copy_ctx(x):
-            ctx_q[x] = work.tile([P, K], BF16, name="ctx_q", tag="ctx_q", bufs=2, align_bytes=64)
+            ctx_words[x] = work.tile([P, K], BF16, name="ctx_q", tag="ctx_q", bufs=3, align_bytes=64)
             nc.scalar.copy(
-                out=ctx_q[x][:].bitcast(F32).rearrange("p (g m u) -> p g m u", g=2, u=2),
+                out=ctx_words[x][:].bitcast(F32).rearrange("p (g m u) -> p g m u", g=2, u=2),
                 in_=ctx_bank[x][:].rearrange("p (g u m) -> p g m u", g=2, u=2),
             )
 
         def quantize_ctx(x):
             codes = work.tile([P, 2 * P], U32, name="ctx_codes", tag="ctx_codes", bufs=3, align_bytes=64)
             scales = work.tile([P, 2 * P], U8, name="ctx_scales", tag="ctx_scales", bufs=3, align_bytes=64)
-            ctx_codes[x] = (codes, scales)
-            nc.vector.quantize_mx(out=codes[:].bitcast(FP8X4), scales=scales[:], in_=ctx_q[x][:])
+            ctx_mx[x] = (codes, scales)
+            nc.vector.quantize_mx(out=codes[:].bitcast(FP8X4), scales=scales[:], in_=ctx_words[x][:])
 
-        def stage1(x, tag="coef"):
+        def prepare_ctx(x, role):
+            turn_ctx(x, role)
+            copy_ctx(x)
+            quantize_ctx(x)
+
+        def stage1(x, role=COEF):
             i = x // TILES_PER_VIEW
-            codes, scales = ctx_codes[x]
-            c_bank[x] = bank(tag)
+            codes, scales = ctx_mx[x]
+            coef_bank[x] = bank(role)
             for g in range(2):
                 nc.tensor.matmul_mx(
-                    out=c_bank[x][:],
+                    out=coef_bank[x][:],
                     lhsT=codes[:, g * P : (g + 1) * P].bitcast(FP8X4),
                     lhsT_scale=scales[:, g * P : (g + 1) * P],
-                    rhs=u_t[i][:, g, :].bitcast(FP4X4),
+                    rhs=u_codes[i][:, g, :].bitcast(FP4X4),
                     rhs_scale=u_plane[:, 2 * i + g, :],
                     start=(g == 0),
                     stop=(g == 1),
@@ -126,278 +180,248 @@ def tile_lowrank_background_foreground_k7_kernel(
         def weigh(x):
             i = x // TILES_PER_VIEW
             h_sorted[x] = work.tile([P, R], BF16, name="h_sorted", tag="h_sorted", bufs=2)
+            weights = d_sorted[:, i].rearrange("m u p -> m (u p)").bitcast(BF16)
             nc.vector.tensor_tensor(
                 out=h_sorted[x][:].rearrange("m (u p e) -> m u p e", u=2, e=2),
-                in0=c_bank[x][:].rearrange("m (p u e) -> m u p e", u=2, e=2),
-                in1=d_sorted[:, i].rearrange("m u p -> m (u p)").bitcast(BF16).rearrange("m (u p e) -> m u p e", u=2, e=2),
+                in0=coef_bank[x][:].rearrange("m (p u e) -> m u p e", u=2, e=2),
+                in1=weights.rearrange("m (u p e) -> m u p e", u=2, e=2),
                 op=ALU.mult,
             )
 
-        def turn_h(x, tag="coef"):
-            h_bank[x] = bank(tag)
-            words = h_sorted[x][:].bitcast(F32)
+        def turn_h(x, role=TURN):
+            h_bank[x] = bank(role)
+            pairs = h_sorted[x][:].bitcast(F32)
             for u in range(2):
-                nc.tensor.transpose(h_bank[x][:, u * P : (u + 1) * P], words[:, u * P : (u + 1) * P], ident[:])
+                nc.tensor.transpose(h_bank[x][:, u * P : (u + 1) * P], pairs[:, u * P : (u + 1) * P], ident[:])
 
         def copy_h(x):
-            h_q[x] = work.tile([P, R], BF16, name="h_q", tag="h_q", bufs=2, align_bytes=64)
+            h_words[x] = work.tile([P, R], BF16, name="h_q", tag="h_q", bufs=2, align_bytes=64)
             nc.scalar.copy(
-                out=h_q[x][:].bitcast(F32).rearrange("p (m u) -> p m u", u=2),
+                out=h_words[x][:].bitcast(F32).rearrange("p (m u) -> p m u", u=2),
                 in_=h_bank[x][:, : 2 * P].rearrange("p (u m) -> p m u", u=2),
             )
 
         def quantize_h(x):
             codes = work.tile([P, P], U32, name="h_codes", tag="h_codes", bufs=6, align_bytes=64)
             scales = work.tile([P, P], U8, name="h_scales", tag="h_scales", bufs=6, align_bytes=64)
-            h_codes[x] = (codes, scales)
-            nc.vector.quantize_mx(out=codes[:].bitcast(FP8X4), scales=scales[:], in_=h_q[x][:])
+            h_mx[x] = (codes, scales)
+            nc.vector.quantize_mx(out=codes[:].bitcast(FP8X4), scales=scales[:], in_=h_words[x][:])
 
         def stage2(s):
             n, g = divmod(s, 2)
             i = n // PAIRS_PER_VIEW
             for j in range(2):
-                codes, scales = h_codes[2 * n + j]
-                l_bank[s, j] = bank("back%d" % j)
+                codes, scales = h_mx[2 * n + j]
+                back_bank[s, j] = bank(BACK[j])
                 nc.tensor.matmul_mx(
-                    out=l_bank[s, j][:],
+                    out=back_bank[s, j][:],
                     lhsT=codes[:].bitcast(FP8X4),
                     lhsT_scale=scales[:],
-                    rhs=v_t[i][:, 2 * KP * g : 2 * KP * (g + 1)].bitcast(FP4X4),
-                    rhs_scale=v_plane[:, i, KP * g : KP * (g + 1)],
+                    rhs=v_codes[i][:, 2 * GROUP * g : 2 * GROUP * (g + 1)].bitcast(FP4X4),
+                    rhs_scale=v_plane[:, i, GROUP * g : GROUP * (g + 1)],
                     start=True,
                     stop=True,
                 )
 
         def residual(s):
             n, g = divmod(s, 2)
-            d_t[s] = work.tile([P, 2, KP], F32, name="resid", tag="resid", bufs=3)
+            resid[s] = work.tile([P, 2, GROUP], F32, name="resid", tag="resid", bufs=3)
             for j in range(2):
+                pixels = frame_pair[n][:, j, GROUP * g : GROUP * (g + 1)]
                 nc.vector.tensor_tensor(
-                    out=d_t[s][:, j, :].rearrange("m (t p) -> m t p", t=4),
-                    in0=frame_t[n][:, j, KP * g : KP * (g + 1)].rearrange("m (p t) -> m t p", t=4),
-                    in1=l_bank[s, j][:].rearrange("m (p t) -> m t p", t=4),
+                    out=resid[s][:, j, :].rearrange("m (t c i) -> m c t i", t=SLOTS, i=4),
+                    in0=pixels.rearrange("m (c i t) -> m c t i", t=SLOTS, i=4),
+                    in1=back_bank[s, j][:].rearrange("m (c i t) -> m c t i", t=SLOTS, i=4),
                     op=ALU.subtract,
                 )
 
-        def turn_residual(s):
+        def turn_residual(s, roles=RESID):
             for h in range(2):
-                dt_bank[s, h] = bank("resid%d" % h)
-                for tt in range(2):
-                    t = 2 * h + tt
+                resid_bank[s, h] = bank(roles[h])
+                for t in (2 * h, 2 * h + 1):
                     for j in range(2):
-                        c0 = tt * PAIR + j * P
+                        c0 = (t % 2) * UNIT_FRAMES + j * P
                         nc.tensor.transpose(
-                            dt_bank[s, h][:, c0 : c0 + P], d_t[s][:, j, t * P : (t + 1) * P], ident[:]
+                            resid_bank[s, h][:, c0 : c0 + P], resid[s][:, j, t * P : (t + 1) * P], ident[:]
                         )
+
+        def turned_resid(s, t):
+            return resid_bank[s, t // 2][:, (t % 2) * UNIT_FRAMES : (t % 2 + 1) * UNIT_FRAMES]
 
         def bound_col(s, t):
             n, g = divmod(s, 2)
-            c = (2 * (n // PAIRS_PER_VIEW) + g) * 4 + t
+            c = (2 * (n // PAIRS_PER_VIEW) + g) * SLOTS + t
             return slice(c, c + 1)
 
-        def above(s, h):
-            if h == 0:
-                r_t[s] = work.tile([P, 4, PAIR], F32, name="above", tag="above", bufs=2)
-            for tt in range(2):
-                t = 2 * h + tt
+        def shared(s):
+            return s < SHARED_UNITS and s % SHARE_PERIOD != SHARE_PERIOD - 1
+
+        def rectify(s):
+            above_hi[s] = work.tile([P, SLOTS, UNIT_FRAMES], F32, name="above", tag="above", bufs=2)
+            for t in range(SLOTS):
                 nc.scalar.activation(
-                    out=r_t[s][:, t, :],
-                    in_=dt_bank[s, h][:, tt * PAIR : (tt + 1) * PAIR],
+                    out=above_hi[s][:, t, :],
+                    in_=turned_resid(s, t),
                     func=ACT.Relu,
                     bias=neg_hi_col[:, bound_col(s, t)],
                 )
+            if shared(s):
+                below_lo[s] = work.tile([P, UNIT_FRAMES], F32, name="below", tag="below", bufs=2)
+                nc.scalar.activation(
+                    out=below_lo[s][:],
+                    in_=turned_resid(s, SLOTS - 1),
+                    func=ACT.Relu,
+                    scale=-1.0,
+                    bias=lo_col[:, bound_col(s, SLOTS - 1)],
+                )
 
         def threshold(s):
-            yt_t[s] = work.tile([P, 4, PAIR], F32, name="yt", tag="yt", bufs=3)
-            for t in range(4):
-                h, tt = divmod(t, 2)
+            y_turned[s] = work.tile([P, SLOTS, UNIT_FRAMES], F32, name="yt", tag="yt", bufs=3)
+            for t in range(SLOTS - 1 if shared(s) else SLOTS):
                 nc.vector.scalar_tensor_tensor(
-                    out=yt_t[s][:, t, :],
-                    in0=dt_bank[s, h][:, tt * PAIR : (tt + 1) * PAIR],
+                    out=y_turned[s][:, t, :],
+                    in0=turned_resid(s, t),
                     scalar=lo_col[:, bound_col(s, t)],
-                    in1=r_t[s][:, t, :],
+                    in1=above_hi[s][:, t, :],
                     op0=ALU.subtract,
                     op1=ALU.min,
                 )
+            if shared(s):
+                t = SLOTS - 1
+                nc.gpsimd.tensor_tensor(
+                    out=y_turned[s][:, t, :], in0=above_hi[s][:, t, :], in1=below_lo[s][:], op=ALU.subtract
+                )
 
         def round_y(s):
-            if s == TILES - 1:
-                yb_t[s] = keep.tile([P, 4 * PAIR], BF16, name="yb_last", align_bytes=64)
-                nc.vector.tensor_copy(
-                    out=yb_t[s][:].rearrange("p (c i t) -> p c t i", t=4, i=4),
-                    in_=yt_t[s][:].rearrange("p t (c i) -> p c t i", i=4),
-                )
-                return
-            yb_t[s] = work.tile([P, 4 * PAIR], BF16, name="yb", tag="yb", bufs=1, align_bytes=64)
+            y_words[s] = work.tile([P, SLOTS * UNIT_FRAMES], BF16, name="yb", tag="yb", bufs=1, align_bytes=64)
             nc.gpsimd.tensor_scalar(
-                out=yb_t[s][:].rearrange("p (m t) -> p m t", t=4),
-                in0=yt_t[s][:].rearrange("p t m -> p m t"),
+                out=y_words[s][:].rearrange("p (m t) -> p m t", t=SLOTS),
+                in0=y_turned[s][:].rearrange("p t m -> p m t"),
                 scalar1=1.0,
                 scalar2=1.0,
                 op0=ALU.mult,
                 op1=ALU.mult,
             )
 
+        def round_last_y(s):
+            y_words[s] = work.tile([P, SLOTS * UNIT_FRAMES], BF16, name="yb_last", tag="yb_last", align_bytes=64)
+            nc.vector.tensor_copy(
+                out=y_words[s][:].rearrange("p (c i t) -> p c t i", t=SLOTS, i=4),
+                in_=y_turned[s][:].rearrange("p t (c i) -> p c t i", i=4),
+            )
+
         def quantize_y(s):
             n, g = divmod(s, 2)
             i, k = divmod(n, PAIRS_PER_VIEW)
             if g == 0:
-                y_codes[n] = work.tile([P, 2, PAIR], U32, name="y_codes", tag="y_codes", bufs=3, align_bytes=64)
+                y_codes[n] = work.tile([P, 2, UNIT_FRAMES], U32, name="y_codes", tag="y_codes", bufs=3, align_bytes=64)
                 if k == 0:
                     y_scales[i] = work.tile([P, 2, T], U8, name="y_scales", tag="y_scales", bufs=2, align_bytes=64)
             nc.vector.quantize_mx(
                 out=y_codes[n][:, g, :].bitcast(FP8X4),
-                scales=y_scales[i][:, g, k * PAIR : (k + 1) * PAIR],
-                in_=yb_t[s][:],
+                scales=y_scales[i][:, g, k * UNIT_FRAMES : (k + 1) * UNIT_FRAMES],
+                in_=y_words[s][:],
             )
 
-        def turn_y(s):
+        def turn_y(s, roles=OUT):
             for j in range(2):
-                y_bank[s, j] = bank("out%d" % j)
-                for t in range(4):
+                out_bank[s, j] = bank(roles[j])
+                for t in range(SLOTS):
                     nc.tensor.transpose(
-                        y_bank[s, j][:, t * P : (t + 1) * P], yt_t[s][:, t, j * P : (j + 1) * P], ident[:]
+                        out_bank[s, j][:, t * P : (t + 1) * P], y_turned[s][:, t, j * P : (j + 1) * P], ident[:]
                     )
 
-        def copy_y(s):
+        def copy_y(s, j, copy=nc.scalar.copy):
             n, g = divmod(s, 2)
-            if g == 0:
-                y_t[n] = work.tile([P, 2, NPIX], F32, name="y", tag="y", bufs=3)
-            for j in range(2):
-                nc.scalar.copy(
-                    out=y_t[n][:, j, KP * g : KP * (g + 1)].rearrange("m (p t) -> m p t", t=4),
-                    in_=y_bank[s, j][:].rearrange("m (t p) -> m p t", t=4),
-                )
+            if g == 0 and j == 0:
+                y_pair[n] = work.tile([P, 2, NPIX], F32, name="y", tag="y", bufs=3)
+            copy(
+                out=y_pair[n][:, j, GROUP * g : GROUP * (g + 1)].rearrange("m (p t) -> m p t", t=SLOTS),
+                in_=out_bank[s, j][:].rearrange("m (t p) -> m p t", t=SLOTS),
+            )
 
         def store_y(s):
             n, g = divmod(s, 2)
-            rows = y_rows[n * PAIR : (n + 1) * PAIR, :].rearrange("(j m) c -> m j c", j=2)
-            cols = slice(KP * g, KP * (g + 1))
-            if s == TILES - 1:
+            rows = y_rows[n * UNIT_FRAMES : (n + 1) * UNIT_FRAMES, :].rearrange("(j m) c -> m j c", j=2)
+            cols = slice(GROUP * g, GROUP * (g + 1))
+            if s >= UNITS - 2:
                 for j in range(2):
-                    nc.sync.dma_start(out=rows[:, j, cols], in_=y_t[n][:, j, cols])
+                    nc.sync.dma_start(out=rows[:, j, cols], in_=y_pair[n][:, j, cols])
             else:
-                nc.sync.dma_start(out=rows[:, :, cols], in_=y_t[n][:, :, cols])
+                nc.sync.dma_start(out=rows[:, :, cols], in_=y_pair[n][:, :, cols])
 
         def store_planes(s):
             n, g = divmod(s, 2)
             i, k = divmod(n, PAIRS_PER_VIEW)
-            words = out_1[:, :, n * PAIR : (n + 1) * PAIR, :].rearrange("g p m t -> p g (m t)").bitcast(I32)
-            if n == TILES // 2 - 1:
+            columns = slice(n * UNIT_FRAMES, (n + 1) * UNIT_FRAMES)
+            words = out_1[:, :, columns, :].rearrange("g p m t -> p g (m t)").bitcast(I32)
+            if s >= UNITS - 2:
                 nc.sync.dma_start(out=words[:, g, :], in_=y_codes[n][:, g, :].bitcast(I32))
             elif g == 1:
                 nc.sync.dma_start(out=words, in_=y_codes[n][:].bitcast(I32))
             if g == 1 and k == PAIRS_PER_VIEW - 1:
-                for q in range(4):
+                for quad in range(4):
+                    scale_rows = out_2[:, 4 * quad : 4 * quad + 4, i * T : (i + 1) * T]
                     nc.sync.dma_start(
-                        out=out_2[:, 4 * q : 4 * q + 4, i * T : (i + 1) * T].rearrange("g r m -> r g m").bitcast(I32),
-                        in_=y_scales[i][32 * q : 32 * q + 4].bitcast(I32),
+                        out=scale_rows.rearrange("g r m -> r g m").bitcast(I32),
+                        in_=y_scales[i][32 * quad : 32 * quad + 4].bitcast(I32),
                     )
 
-        def spread_d(u):
-            words = d_rows[:].bitcast(F32)
-            if True:
-                b = bank("out%d" % u)
-                for a in range(4):
-                    c = 2 * a + u
-                    nc.tensor.transpose(b[:, a * P : (a + 1) * P], words[:, c : c + 1].to_broadcast([P, P]), ident[:])
-                nc.scalar.copy(
-                    out=d_sorted[:, :, u, :].rearrange("q i (b a) -> q i b a", a=4),
-                    in_=b[:].rearrange("q (a i b) -> q i b a", a=4, i=G),
-                )
+        def when(step, x, *more):
+            if 0 <= x < TILES:
+                step(x, *more)
 
-        def turn_bounds():
-            words = bound_rows[:].bitcast(F32)
-            b = bank("out1")
-            for u in range(2):
-                nc.tensor.transpose(b[:, u * P : (u + 1) * P], words[:, u : 256 : 2], ident[:])
-            values = b[:, : 2 * P].bitcast(BF16).rearrange("p (u r e) -> p r u e", u=2, e=2)
-            nc.scalar.activation(
-                out=neg_hi_col[:].rearrange("p (r u e) -> p r u e", u=2, e=2),
-                in_=values[:, 8:16], func=ACT.Identity, scale=-1.0,
-            )
-            nc.scalar.activation(
-                out=lo_col[:].rearrange("p (r u e) -> p r u e", u=2, e=2), in_=values[:, 0:8], func=ACT.Identity
-            )
-
-        nc.vector.memset(bound_rows[:], 0.0)
+        nc.gpsimd.memset(bound_rows[:].bitcast(I32), 0)
         make_identity(nc, ident[:])
         nc.vector.memset(u_plane[:].bitcast(I32), 0)
         nc.vector.memset(v_plane[:].bitcast(I32), 0)
 
-        def load_d():
-            nc.sync.dma_start(out=d_rows[:], in_=d.rearrange("i (b c) -> (i b) c", c=16))
-
-        def load_bounds():
-            nc.sync.dma_start(out=bound_rows[0:8, :], in_=lo.rearrange("i (g c) -> (i g) c", g=2))
-            nc.sync.dma_start(out=bound_rows[8:16, :], in_=hi.rearrange("i (g c) -> (i g) c", g=2))
-
-        def when(f, x, *more):
-            if 0 <= x < TILES:
-                f(x, *more)
-
-        def prepare_ctx(x, tag):
-            turn_ctx(x, 0, tag)
-            turn_ctx(x, 1)
-            copy_ctx(x)
-            quantize_ctx(x)
-
-        def finish_h(x, tag):
-            turn_h(x, tag)
-            copy_h(x)
-            quantize_h(x)
-
-        load_d()
-        load_bounds()
         load_ctx(0)
+        load_bounds()
+        load_d(d_first, slice(0, 1))
         load_ctx(1)
+        load_ctx(2)
         load_plane(u_plane, u_scales)
         load_u(0)
-        load_ctx(2)
         load_ctx(3)
         load_plane(v_plane, v_scales)
         load_v(0)
         load_ctx(4)
         load_frames(0)
+        load_d(d_rest, slice(1, G))
 
         turn_bounds()
-        prepare_ctx(0, "turn")
-        spread_d(0)
-        prepare_ctx(1, "resid0")
-        stage1(0, "coef")
-        spread_d(1)
-        turn_ctx(2, 0, "turn")
-        turn_ctx(2, 1)
+        prepare_ctx(0, TURN)
+        spread_d(0, 1, d_first, 0, BACK[1])
+        prepare_ctx(1, RESID[0])
+        prepare_ctx(2, RESID[1])
         load_ctx(5)
-        stage1(1, "back0")
+        stage1(0)
+        stage1(1, BACK[0])
         weigh(0)
-        copy_ctx(2)
-        quantize_ctx(2)
-        turn_h(0, "out0")
-        turn_ctx(3, 0, "resid0")
-        turn_ctx(3, 1)
+        weigh(1)
+        turn_ctx(3)
         load_ctx(6)
         load_frames(1)
-        weigh(1)
-        copy_h(0)
-        quantize_h(0)
+        turn_h(0, OUT[0])
         copy_ctx(3)
+        copy_h(0)
         quantize_ctx(3)
-        stage1(2, "coef")
-        turn_h(1, "out0")
-        turn_ctx(4, 0, "turn")
-        turn_ctx(4, 1)
+        quantize_h(0)
+        stage1(2)
+        turn_h(1, OUT[1])
+        turn_ctx(4, RESID[0])
         load_ctx(7)
-        weigh(2)
         copy_h(1)
         quantize_h(1)
+        weigh(2)
         copy_ctx(4)
         quantize_ctx(4)
-        stage1(3, "out1")
+        stage1(3, OUT[1])
         stage2(0)
-        turn_h(2, "out0")
-        turn_ctx(5, 0, "turn")
-        turn_ctx(5, 1)
+        turn_h(2, OUT[0])
+        turn_ctx(5)
+        turn_ctx(6, RESID[1])
         load_ctx(8)
         load_u(1)
         load_frames(2)
@@ -405,39 +429,42 @@ def tile_lowrank_background_foreground_k7_kernel(
         weigh(3)
         copy_h(2)
         copy_ctx(5)
+        copy_ctx(6)
         stage1(4)
         stage2(1)
+        turn_h(3, OUT[1])
         turn_residual(0)
-        turn_h(3, "out1")
-        turn_ctx(6, 0)
-        above(0, 0)
         copy_h(3)
-        above(0, 1)
+        rectify(0)
         quantize_h(2)
         residual(1)
         quantize_h(3)
         quantize_ctx(5)
+        stage2(2)
+        spread_d(1, 2, d_rest, 0, OUT[0])
+        spread_d(3, 1, d_rest, 2, OUT[1])
 
-        for s in range(TILES):
-            when(threshold, s)
-            when(round_y, s - 1)
-            when(turn_y, s - 1)
-            when(turn_ctx, s + 6, 1)
-            when(copy_y, s - 1)
+        for s in range(UNITS - 2):
+            borrow = s + 1 >= UNITS - 3 and s % 2 == 0
             when(weigh, s + 4)
-            when(stage2, s + 2)
-            when(copy_ctx, s + 6)
+            when(round_y, s - 1)
+            if s > 0:
+                when(copy_ctx, s + 6)
+            threshold(s)
+            when(copy_y, s - 1, 0)
+            when(copy_y, s - 1, 1)
             when(turn_h, s + 4)
             when(copy_h, s + 4)
-            when(residual, s + 2)
-            when(turn_residual, s + 1)
-            when(turn_ctx, s + 7, 0)
-            when(above, s + 1, 0)
-            when(above, s + 1, 1)
+            turn_residual(s + 1, (COEF, TURN) if borrow else RESID)
+            rectify(s + 1)
+            when(stage1, s + 5)
+            residual(s + 2)
+            when(turn_ctx, s + 7)
+            turn_y(s)
             when(quantize_h, s + 4)
             when(quantize_ctx, s + 6)
             when(quantize_y, s - 1)
-            when(stage1, s + 5)
+            when(stage2, s + 3)
             when(load_ctx, s + 9)
             if s % 2 == 0 and s + 6 < TILES:
                 load_frames((s + 6) // 2)
@@ -447,10 +474,29 @@ def tile_lowrank_background_foreground_k7_kernel(
                 load_v((s + 6) // TILES_PER_VIEW)
             when(store_y, s - 1)
             when(store_planes, s - 1)
-        last = TILES - 1
-        turn_y(last)
-        round_y(last)
-        copy_y(last)
+
+        last = UNITS - 1
+        round_y(last - 2)
+        turn_residual(last, (COEF, TURN))
+        threshold(last - 1)
+        copy_y(last - 2, 0)
+        rectify(last)
+        copy_y(last - 2, 1, nc.vector.tensor_copy)
+        store_y(last - 2)
+        turn_y(last - 1, BACK)
+        quantize_y(last - 2)
+        store_planes(last - 2)
+        round_y(last - 1)
+        threshold(last)
+        copy_y(last - 1, 0)
+        copy_y(last - 1, 1)
+        store_y(last - 1)
+        turn_y(last, RESID)
+        quantize_y(last - 1)
+        store_planes(last - 1)
+        copy_y(last, 0)
+        round_last_y(last)
+        copy_y(last, 1)
         quantize_y(last)
         store_y(last)
         store_planes(last)

from contextlib import ExitStack

import concourse.mybir as mybir
from concourse.masks import make_identity

G, T, K, R, NPIX = 4, 768, 1024, 512, 1024
FLOPS = 2 * G * T * K * R + 2 * G * T * R * NPIX

F32 = mybir.dt.float32
BF16 = mybir.dt.bfloat16
I32 = mybir.dt.int32
U32 = mybir.dt.uint32
U8 = mybir.dt.uint8
FP8X4 = mybir.dt.float8_e4m3fn_x4
FP4X4 = mybir.dt.float4_e2m1fn_x4
ALU = mybir.AluOpType
ACT = mybir.ActivationFunctionType

P = 128
GROUP = 512
SLOTS = 4
UNIT_FRAMES = 2 * P
TILES = G * T // P
UNITS = TILES
TILES_PER_VIEW = T // P
PAIRS_PER_VIEW = T // UNIT_FRAMES
BOUND_ROWS = 2 * G

SHARED_UNITS = 19
SHARE_PERIOD = 4

TURN, COEF = "turn", "coef"
BACK = ("back0", "back1")
RESID = ("resid0", "resid1")
OUT = ("out0", "out1")


def tile_lowrank_background_foreground_k7_kernel(
    tc, context, u_words, u_scales, d, v_words, v_scales, frames, lo, hi, out_0, out_1, out_2
):
    nc = tc.nc
    ctx_rows = context.rearrange("i f k -> (i f) k")
    frame_rows = frames.rearrange("i f k -> (i f) k")
    y_rows = out_0.rearrange("i f k -> (i f) k")

    with ExitStack() as stack:
        keep = stack.enter_context(tc.tile_pool(name="keep", bufs=1))
        work = stack.enter_context(tc.tile_pool(name="work", bufs=2))
        psum = stack.enter_context(tc.psum_pool(name="psum", bufs=1))
        stack.enter_context(tc.manual_schedule())

        def bank(role):
            return psum.tile([P, GROUP], F32, name=role, tag=role)

        ident = keep.tile([P, P], F32, name="ident")
        u_plane = keep.tile([P, 2 * G, R], U8, name="u_plane", align_bytes=64)
        v_plane = keep.tile([P, G, NPIX], U8, name="v_plane", align_bytes=64)
        d_first = keep.tile([P, 1, SLOTS], BF16, name="d_first")
        d_rest = keep.tile([P, G - 1, SLOTS], BF16, name="d_rest")
        d_sorted = keep.tile([P, G, 2, P], F32, name="d_sorted")
        bound_rows = keep.tile([P, GROUP], BF16, name="bound_rows")
        lo_col = keep.tile([P, BOUND_ROWS * SLOTS], F32, name="lo_col")
        neg_hi_col = keep.tile([P, BOUND_ROWS * SLOTS], F32, name="neg_hi_col")

        ctx_raw, ctx_bank, ctx_words, ctx_mx = {}, {}, {}, {}
        u_codes, v_codes, frame_pair = {}, {}, {}
        coef_bank, h_sorted, h_bank, h_words, h_mx = {}, {}, {}, {}, {}
        back_bank, resid, resid_bank, above_hi, below_lo = {}, {}, {}, {}, {}
        y_turned, y_words, out_bank, y_pair, y_codes, y_scales = {}, {}, {}, {}, {}, {}

        def load_ctx(x):
            ctx_raw[x] = work.tile([P, K], BF16, name="ctx", tag="ctx", bufs=5)
            nc.sync.dma_start(out=ctx_raw[x][:], in_=ctx_rows[x * P : (x + 1) * P, :])

        def load_u(i):
            u_codes[i] = work.tile([P, 2, 2 * R], U8, name="u", tag="u", bufs=2, align_bytes=64)
            nc.sync.dma_start(
                out=u_codes[i][:].bitcast(I32),
                in_=u_words[2 * i : 2 * i + 2].rearrange("g p n -> p g n").bitcast(I32),
            )

        def load_v(i):
            v_codes[i] = work.tile([P, 2 * NPIX], U8, name="v", tag="v", bufs=2, align_bytes=64)
            nc.sync.dma_start(out=v_codes[i][:].bitcast(I32), in_=v_words[i].bitcast(I32))

        def load_frames(n):
            frame_pair[n] = work.tile([P, 2, NPIX], BF16, name="frames", tag="frames", bufs=3)
            nc.sync.dma_start(
                out=frame_pair[n][:],
                in_=frame_rows[n * UNIT_FRAMES : (n + 1) * UNIT_FRAMES, :].rearrange("(j m) c -> m j c", j=2),
            )

        def load_plane(plane, scales):
            for quad in range(4):
                nc.sync.dma_start(
                    out=plane[32 * quad : 32 * quad + 4].bitcast(I32),
                    in_=scales[:, 4 * quad : 4 * quad + 4, :].rearrange("g r n -> r g n").bitcast(I32),
                )

        def load_d(rows, views):
            nc.sync.dma_start(out=rows[:], in_=d[views].rearrange("i (p c) -> p i c", c=SLOTS))

        def load_bounds():
            nc.sync.dma_start(out=bound_rows[:BOUND_ROWS, :], in_=lo.rearrange("i (g c) -> (i g) c", g=2))
            nc.sync.dma_start(
                out=bound_rows[BOUND_ROWS : 2 * BOUND_ROWS, :], in_=hi.rearrange("i (g c) -> (i g) c", g=2)
            )

        def spread_d(view, count, rows, first_row, role):
            pairs = rows[:].rearrange("p i c -> p (i c)").bitcast(F32)
            spread = bank(role)
            for c in range(2 * count):
                w = 2 * first_row + c
                nc.tensor.transpose(spread[:, c * P : (c + 1) * P], pairs[:, w : w + 1].to_broadcast([P, P]), ident[:])
            nc.scalar.copy(
                out=d_sorted[:, view : view + count].rearrange("q i u p -> q (i u p)"), in_=spread[:, : 2 * count * P]
            )

        def turn_bounds():
            pairs = bound_rows[:].bitcast(F32)
            turned = bank(OUT[1])
            for u in range(2):
                nc.tensor.transpose(turned[:, u * P : (u + 1) * P], pairs[:, u : GROUP // 2 : 2], ident[:])
            values = turned[:, : 2 * P].bitcast(BF16).rearrange("p (u r e) -> p r u e", u=2, e=2)
            nc.scalar.activation(
                out=neg_hi_col[:].rearrange("p (r u e) -> p r u e", u=2, e=2),
                in_=values[:, BOUND_ROWS : 2 * BOUND_ROWS],
                func=ACT.Identity,
                scale=-1.0,
            )
            nc.scalar.activation(
                out=lo_col[:].rearrange("p (r u e) -> p r u e", u=2, e=2),
                in_=values[:, :BOUND_ROWS],
                func=ACT.Identity,
            )

        def turn_ctx(x, role=TURN):
            ctx_bank[x] = bank(role)
            pairs = ctx_raw[x][:].bitcast(F32)
            for g in range(2):
                for u in range(2):
                    c0 = (2 * g + u) * P
                    nc.tensor.transpose(
                        ctx_bank[x][:, c0 : c0 + P], pairs[:, 2 * P * g + u : 2 * P * (g + 1) : 2], ident[:]
                    )

        def copy_ctx(x):
            ctx_words[x] = work.tile([P, K], BF16, name="ctx_q", tag="ctx_q", bufs=3, align_bytes=64)
            nc.scalar.copy(
                out=ctx_words[x][:].bitcast(F32).rearrange("p (g m u) -> p g m u", g=2, u=2),
                in_=ctx_bank[x][:].rearrange("p (g u m) -> p g m u", g=2, u=2),
            )

        def quantize_ctx(x):
            codes = work.tile([P, 2 * P], U32, name="ctx_codes", tag="ctx_codes", bufs=3, align_bytes=64)
            scales = work.tile([P, 2 * P], U8, name="ctx_scales", tag="ctx_scales", bufs=3, align_bytes=64)
            ctx_mx[x] = (codes, scales)
            nc.vector.quantize_mx(out=codes[:].bitcast(FP8X4), scales=scales[:], in_=ctx_words[x][:])

        def prepare_ctx(x, role):
            turn_ctx(x, role)
            copy_ctx(x)
            quantize_ctx(x)

        def stage1(x, role=COEF):
            i = x // TILES_PER_VIEW
            codes, scales = ctx_mx[x]
            coef_bank[x] = bank(role)
            for g in range(2):
                nc.tensor.matmul_mx(
                    out=coef_bank[x][:],
                    lhsT=codes[:, g * P : (g + 1) * P].bitcast(FP8X4),
                    lhsT_scale=scales[:, g * P : (g + 1) * P],
                    rhs=u_codes[i][:, g, :].bitcast(FP4X4),
                    rhs_scale=u_plane[:, 2 * i + g, :],
                    start=(g == 0),
                    stop=(g == 1),
                )

        def weigh(x):
            i = x // TILES_PER_VIEW
            h_sorted[x] = work.tile([P, R], BF16, name="h_sorted", tag="h_sorted", bufs=2)
            weights = d_sorted[:, i].rearrange("m u p -> m (u p)").bitcast(BF16)
            nc.vector.tensor_tensor(
                out=h_sorted[x][:].rearrange("m (u p e) -> m u p e", u=2, e=2),
                in0=coef_bank[x][:].rearrange("m (p u e) -> m u p e", u=2, e=2),
                in1=weights.rearrange("m (u p e) -> m u p e", u=2, e=2),
                op=ALU.mult,
            )

        def turn_h(x, role=TURN):
            h_bank[x] = bank(role)
            pairs = h_sorted[x][:].bitcast(F32)
            for u in range(2):
                nc.tensor.transpose(h_bank[x][:, u * P : (u + 1) * P], pairs[:, u * P : (u + 1) * P], ident[:])

        def copy_h(x):
            h_words[x] = work.tile([P, R], BF16, name="h_q", tag="h_q", bufs=2, align_bytes=64)
            nc.scalar.copy(
                out=h_words[x][:].bitcast(F32).rearrange("p (m u) -> p m u", u=2),
                in_=h_bank[x][:, : 2 * P].rearrange("p (u m) -> p m u", u=2),
            )

        def quantize_h(x):
            codes = work.tile([P, P], U32, name="h_codes", tag="h_codes", bufs=6, align_bytes=64)
            scales = work.tile([P, P], U8, name="h_scales", tag="h_scales", bufs=6, align_bytes=64)
            h_mx[x] = (codes, scales)
            nc.vector.quantize_mx(out=codes[:].bitcast(FP8X4), scales=scales[:], in_=h_words[x][:])

        def stage2(s):
            n, g = divmod(s, 2)
            i = n // PAIRS_PER_VIEW
            for j in range(2):
                codes, scales = h_mx[2 * n + j]
                back_bank[s, j] = bank(BACK[j])
                nc.tensor.matmul_mx(
                    out=back_bank[s, j][:],
                    lhsT=codes[:].bitcast(FP8X4),
                    lhsT_scale=scales[:],
                    rhs=v_codes[i][:, 2 * GROUP * g : 2 * GROUP * (g + 1)].bitcast(FP4X4),
                    rhs_scale=v_plane[:, i, GROUP * g : GROUP * (g + 1)],
                    start=True,
                    stop=True,
                )

        def residual(s):
            n, g = divmod(s, 2)
            resid[s] = work.tile([P, 2, GROUP], F32, name="resid", tag="resid", bufs=3)
            for j in range(2):
                pixels = frame_pair[n][:, j, GROUP * g : GROUP * (g + 1)]
                nc.vector.tensor_tensor(
                    out=resid[s][:, j, :].rearrange("m (t c i) -> m c t i", t=SLOTS, i=4),
                    in0=pixels.rearrange("m (c i t) -> m c t i", t=SLOTS, i=4),
                    in1=back_bank[s, j][:].rearrange("m (c i t) -> m c t i", t=SLOTS, i=4),
                    op=ALU.subtract,
                )

        def turn_residual(s, roles=RESID):
            for h in range(2):
                resid_bank[s, h] = bank(roles[h])
                for t in (2 * h, 2 * h + 1):
                    for j in range(2):
                        c0 = (t % 2) * UNIT_FRAMES + j * P
                        nc.tensor.transpose(
                            resid_bank[s, h][:, c0 : c0 + P], resid[s][:, j, t * P : (t + 1) * P], ident[:]
                        )

        def turned_resid(s, t):
            return resid_bank[s, t // 2][:, (t % 2) * UNIT_FRAMES : (t % 2 + 1) * UNIT_FRAMES]

        def bound_col(s, t):
            n, g = divmod(s, 2)
            c = (2 * (n // PAIRS_PER_VIEW) + g) * SLOTS + t
            return slice(c, c + 1)

        def shared(s):
            return s < SHARED_UNITS and s % SHARE_PERIOD != SHARE_PERIOD - 1

        def rectify(s):
            above_hi[s] = work.tile([P, SLOTS, UNIT_FRAMES], F32, name="above", tag="above", bufs=2)
            for t in range(SLOTS):
                nc.scalar.activation(
                    out=above_hi[s][:, t, :],
                    in_=turned_resid(s, t),
                    func=ACT.Relu,
                    bias=neg_hi_col[:, bound_col(s, t)],
                )
            if shared(s):
                below_lo[s] = work.tile([P, UNIT_FRAMES], F32, name="below", tag="below", bufs=2)
                nc.scalar.activation(
                    out=below_lo[s][:],
                    in_=turned_resid(s, SLOTS - 1),
                    func=ACT.Relu,
                    scale=-1.0,
                    bias=lo_col[:, bound_col(s, SLOTS - 1)],
                )

        def threshold(s):
            y_turned[s] = work.tile([P, SLOTS, UNIT_FRAMES], F32, name="yt", tag="yt", bufs=3)
            for t in range(SLOTS - 1 if shared(s) else SLOTS):
                nc.vector.scalar_tensor_tensor(
                    out=y_turned[s][:, t, :],
                    in0=turned_resid(s, t),
                    scalar=lo_col[:, bound_col(s, t)],
                    in1=above_hi[s][:, t, :],
                    op0=ALU.subtract,
                    op1=ALU.min,
                )
            if shared(s):
                t = SLOTS - 1
                nc.gpsimd.tensor_tensor(
                    out=y_turned[s][:, t, :], in0=above_hi[s][:, t, :], in1=below_lo[s][:], op=ALU.subtract
                )

        def round_y(s):
            y_words[s] = work.tile([P, SLOTS * UNIT_FRAMES], BF16, name="yb", tag="yb", bufs=1, align_bytes=64)
            nc.gpsimd.tensor_scalar(
                out=y_words[s][:].rearrange("p (m t) -> p m t", t=SLOTS),
                in0=y_turned[s][:].rearrange("p t m -> p m t"),
                scalar1=1.0,
                scalar2=1.0,
                op0=ALU.mult,
                op1=ALU.mult,
            )

        def round_last_y(s):
            y_words[s] = work.tile([P, SLOTS * UNIT_FRAMES], BF16, name="yb_last", tag="yb_last", align_bytes=64)
            nc.vector.tensor_copy(
                out=y_words[s][:].rearrange("p (c i t) -> p c t i", t=SLOTS, i=4),
                in_=y_turned[s][:].rearrange("p t (c i) -> p c t i", i=4),
            )

        def quantize_y(s):
            n, g = divmod(s, 2)
            i, k = divmod(n, PAIRS_PER_VIEW)
            if g == 0:
                y_codes[n] = work.tile([P, 2, UNIT_FRAMES], U32, name="y_codes", tag="y_codes", bufs=3, align_bytes=64)
                if k == 0:
                    y_scales[i] = work.tile([P, 2, T], U8, name="y_scales", tag="y_scales", bufs=2, align_bytes=64)
            nc.vector.quantize_mx(
                out=y_codes[n][:, g, :].bitcast(FP8X4),
                scales=y_scales[i][:, g, k * UNIT_FRAMES : (k + 1) * UNIT_FRAMES],
                in_=y_words[s][:],
            )

        def turn_y(s, roles=OUT):
            for j in range(2):
                out_bank[s, j] = bank(roles[j])
                for t in range(SLOTS):
                    nc.tensor.transpose(
                        out_bank[s, j][:, t * P : (t + 1) * P], y_turned[s][:, t, j * P : (j + 1) * P], ident[:]
                    )

        def copy_y(s, j, copy=nc.scalar.copy):
            n, g = divmod(s, 2)
            if g == 0 and j == 0:
                y_pair[n] = work.tile([P, 2, NPIX], F32, name="y", tag="y", bufs=3)
            copy(
                out=y_pair[n][:, j, GROUP * g : GROUP * (g + 1)].rearrange("m (p t) -> m p t", t=SLOTS),
                in_=out_bank[s, j][:].rearrange("m (t p) -> m p t", t=SLOTS),
            )

        def store_y(s):
            n, g = divmod(s, 2)
            rows = y_rows[n * UNIT_FRAMES : (n + 1) * UNIT_FRAMES, :].rearrange("(j m) c -> m j c", j=2)
            cols = slice(GROUP * g, GROUP * (g + 1))
            if s >= UNITS - 2:
                for j in range(2):
                    nc.sync.dma_start(out=rows[:, j, cols], in_=y_pair[n][:, j, cols])
            else:
                nc.sync.dma_start(out=rows[:, :, cols], in_=y_pair[n][:, :, cols])

        def store_planes(s):
            n, g = divmod(s, 2)
            i, k = divmod(n, PAIRS_PER_VIEW)
            columns = slice(n * UNIT_FRAMES, (n + 1) * UNIT_FRAMES)
            words = out_1[:, :, columns, :].rearrange("g p m t -> p g (m t)").bitcast(I32)
            if s >= UNITS - 2:
                nc.sync.dma_start(out=words[:, g, :], in_=y_codes[n][:, g, :].bitcast(I32))
            elif g == 1:
                nc.sync.dma_start(out=words, in_=y_codes[n][:].bitcast(I32))
            if g == 1 and k == PAIRS_PER_VIEW - 1:
                for quad in range(4):
                    scale_rows = out_2[:, 4 * quad : 4 * quad + 4, i * T : (i + 1) * T]
                    nc.sync.dma_start(
                        out=scale_rows.rearrange("g r m -> r g m").bitcast(I32),
                        in_=y_scales[i][32 * quad : 32 * quad + 4].bitcast(I32),
                    )

        def when(step, x, *more):
            if 0 <= x < TILES:
                step(x, *more)

        nc.gpsimd.memset(bound_rows[:].bitcast(I32), 0)
        make_identity(nc, ident[:])
        nc.vector.memset(u_plane[:].bitcast(I32), 0)
        nc.vector.memset(v_plane[:].bitcast(I32), 0)

        load_ctx(0)
        load_bounds()
        load_d(d_first, slice(0, 1))
        load_ctx(1)
        load_ctx(2)
        load_plane(u_plane, u_scales)
        load_u(0)
        load_ctx(3)
        load_plane(v_plane, v_scales)
        load_v(0)
        load_ctx(4)
        load_frames(0)
        load_d(d_rest, slice(1, G))

        turn_bounds()
        prepare_ctx(0, TURN)
        spread_d(0, 1, d_first, 0, BACK[1])
        prepare_ctx(1, RESID[0])
        prepare_ctx(2, RESID[1])
        load_ctx(5)
        stage1(0)
        stage1(1, BACK[0])
        weigh(0)
        weigh(1)
        turn_ctx(3)
        load_ctx(6)
        load_frames(1)
        turn_h(0, OUT[0])
        copy_ctx(3)
        copy_h(0)
        quantize_ctx(3)
        quantize_h(0)
        stage1(2)
        turn_h(1, OUT[1])
        turn_ctx(4, RESID[0])
        load_ctx(7)
        copy_h(1)
        quantize_h(1)
        weigh(2)
        copy_ctx(4)
        quantize_ctx(4)
        stage1(3, OUT[1])
        stage2(0)
        turn_h(2, OUT[0])
        turn_ctx(5)
        turn_ctx(6, RESID[1])
        load_ctx(8)
        load_u(1)
        load_frames(2)
        residual(0)
        weigh(3)
        copy_h(2)
        copy_ctx(5)
        copy_ctx(6)
        stage1(4)
        stage2(1)
        turn_h(3, OUT[1])
        turn_residual(0)
        copy_h(3)
        rectify(0)
        quantize_h(2)
        residual(1)
        quantize_h(3)
        quantize_ctx(5)
        stage2(2)
        spread_d(1, 2, d_rest, 0, OUT[0])
        spread_d(3, 1, d_rest, 2, OUT[1])

        for s in range(UNITS - 2):
            borrow = s + 1 >= UNITS - 3 and s % 2 == 0
            when(weigh, s + 4)
            when(round_y, s - 1)
            if s > 0:
                when(copy_ctx, s + 6)
            threshold(s)
            when(copy_y, s - 1, 0)
            when(copy_y, s - 1, 1)
            when(turn_h, s + 4)
            when(copy_h, s + 4)
            turn_residual(s + 1, (COEF, TURN) if borrow else RESID)
            rectify(s + 1)
            when(stage1, s + 5)
            residual(s + 2)
            when(turn_ctx, s + 7)
            turn_y(s)
            when(quantize_h, s + 4)
            when(quantize_ctx, s + 6)
            when(quantize_y, s - 1)
            when(stage2, s + 3)
            when(load_ctx, s + 9)
            if s % 2 == 0 and s + 6 < TILES:
                load_frames((s + 6) // 2)
            if (s + 9) % TILES_PER_VIEW == 0 and s + 9 < TILES:
                load_u((s + 9) // TILES_PER_VIEW)
            if (s + 6) % TILES_PER_VIEW == 0 and s + 6 < TILES:
                load_v((s + 6) // TILES_PER_VIEW)
            when(store_y, s - 1)
            when(store_planes, s - 1)

        last = UNITS - 1
        round_y(last - 2)
        turn_residual(last, (COEF, TURN))
        threshold(last - 1)
        copy_y(last - 2, 0)
        rectify(last)
        copy_y(last - 2, 1, nc.vector.tensor_copy)
        store_y(last - 2)
        turn_y(last - 1, BACK)
        quantize_y(last - 2)
        store_planes(last - 2)
        round_y(last - 1)
        threshold(last)
        copy_y(last - 1, 0)
        copy_y(last - 1, 1)
        store_y(last - 1)
        turn_y(last, RESID)
        quantize_y(last - 1)
        store_planes(last - 1)
        copy_y(last, 0)
        round_last_y(last)
        copy_y(last, 1)
        quantize_y(last)
        store_y(last)
        store_planes(last)
